import numpy as np
import ml_dtypes


def mxq(x, axis, fmt="e4m3"):
    dtype, down = {"e4m3": (ml_dtypes.float8_e4m3fn, 7), "e5m2": (ml_dtypes.float8_e5m2, 14)}[fmt]
    v = np.moveaxis(np.asarray(x, np.float32).astype(ml_dtypes.bfloat16).astype(np.float64), axis, -1)
    blocks = v.reshape(v.shape[:-1] + (-1, 32))
    amax = np.abs(blocks).max(-1, keepdims=True)
    byte = np.maximum(np.where(amax > 0, np.frexp(amax)[1] - 1 + 127, 0) - down, 1)
    scale = np.exp2(byte - 127.0)
    codes = (blocks / scale).astype(np.float32).astype(dtype).astype(np.float64)
    return np.moveaxis((codes * scale).reshape(v.shape), -1, axis)


WIDE = False


def mx_kscale(k):
    if not WIDE:
        return np.ones(k)
    levels = np.array([10, -10, 5, -5, 0])
    if k % 512:
        return np.exp2(np.random.permutation(np.resize(levels, k // 32))).repeat(32)
    a = np.empty((k // 512, 16))
    for p in range(k // 512):
        a[p, :8] = np.random.permutation(np.resize(levels, 8))
        for g in range(8):
            far = levels[np.abs(levels - a[p, g]) >= 10]
            a[p, g + 8] = far[np.random.randint(len(far))]
    return np.exp2(a.ravel()).repeat(32)


def f64(x):
    return np.asarray(x).astype(np.float64)


def striped(idx):
    return np.tile(idx.reshape(-1, 16).T, (8, 1)).astype(np.uint16)


def unstriped(offs):
    return offs[:16].T.reshape(-1).astype(np.int64)


E2M1 = np.array([0.0, 0.5, 1.0, 1.5, 2.0, 3.0, 4.0, 6.0, -0.0, -0.5, -1.0, -1.5, -2.0, -3.0, -4.0, -6.0])


def pack_weight(w, fmt):
    k, n = w.shape
    w = f64(np.asarray(w, np.float32).astype(ml_dtypes.bfloat16)).reshape(k // 32, 32, n)
    amax = np.abs(w).max(1)
    if fmt == "e4m3":
        byte = np.frexp(amax)[1] - 1 + 127 - 7
    else:
        mant, ex = np.frexp(amax / 6.0)
        byte = np.where(mant > 0.5, ex, ex - 1) + 127
    byte = np.clip(np.where(amax > 0, byte, 1), 1, 254)
    scaled = (w * np.exp2(127.0 - byte)[:, None, :]).reshape(k, n).astype(np.float32)
    by_word = np.ascontiguousarray(scaled.reshape(k // 512, 128, 4, n).transpose(0, 1, 3, 2))
    if fmt == "e4m3":
        words = by_word.astype(ml_dtypes.float8_e4m3fn).view(np.uint8)
    else:
        c = by_word.astype(ml_dtypes.float4_e2m1fn).view(np.uint8) & 0xF
        words = (c[..., 0::2] | (c[..., 1::2] << 4)).reshape(k // 512, 128, 2 * n)
    return np.ascontiguousarray(words), np.ascontiguousarray(byte.astype(np.uint8).reshape(k // 512, 16, n))


def unpack_weight(words, scales, fmt):
    g, _, n = scales.shape
    words = np.ascontiguousarray(words).reshape(g, 128, n, -1)
    if fmt == "e4m3":
        vals = words.view(ml_dtypes.float8_e4m3fn).astype(np.float64)
    else:
        nib = np.empty((g, 128, n, 4), np.uint8)
        nib[..., 0::2] = words & 0xF
        nib[..., 1::2] = words >> 4
        vals = E2M1[nib]
    vals = vals * np.repeat(np.exp2(scales.astype(np.float64) - 127.0), 8, axis=1)[..., None]
    return vals.transpose(0, 1, 3, 2).reshape(g * 512, n)


def pack_table(v):
    words, scales = pack_weight(v, "e4m3")
    return np.concatenate([words.reshape(words.shape[0], -1), scales.reshape(scales.shape[0], -1)], axis=1)


def unpack_table(tab):
    g, t = tab.shape[0], tab.shape[1] // 528
    return unpack_weight(tab[:, :512 * t].reshape(g, 128, t, 4), tab[:, 512 * t:].reshape(g, 16, t), "e4m3")


K, H, M, T, S = 1536, 512, 1024, 4096, 2048


def setup_inputs():
    n = np.random.standard_normal
    s = mx_kscale(K)[:, None]
    u = mx_kscale(H)[:, None]
    p_w2 = pack_weight(1.4 * n((H, M)) / np.sqrt(H) / u, "e2m1")
    return {
        "tab": pack_table(n((K, T)) * s),
        "w1": (n((K, H)) / np.sqrt(K) / s * u.T).astype(np.float32),
        "w2_words": p_w2[0],
        "w2_scales": p_w2[1],
        "offs": striped(np.random.permutation(T)[:S]),
    }


def reference(tab, w1, w2_words, w2_scales, offs):
    tab_ = unpack_table(tab)[:, unstriped(offs)]
    w1_ = mxq(f64(w1), 0, "e4m3")
    w2_ = unpack_weight(w2_words, w2_scales, "e2m1")
    h_ = mxq(np.maximum(w1_.T @ tab_, 0.0), 0, "e4m3")
    y = h_.T @ w2_
    return y

@@ -1,0 +1,195 @@
+from contextlib import ExitStack
+
+import concourse.mybir as mybir
+
+K, H, M, T, S = 1536, 512, 1024, 4096, 2048
+FLOPS = 2 * S * (K * H + H * M)
+
+F32 = mybir.dt.float32
+BF16 = mybir.dt.bfloat16
+I32 = mybir.dt.int32
+U32 = mybir.dt.uint32
+U16 = mybir.dt.uint16
+U8 = mybir.dt.uint8
+E4M3 = mybir.dt.float8_e4m3fn_x4
+E2M1 = mybir.dt.float4_e2m1fn_x4
+RELU = mybir.ActivationFunctionType.Relu
+
+P = 128
+PASSES = K // 512
+SL = 512
+JT = 128
+
+
+def tile_list_tabmlp_tm_none_kernel(tc, tab, w1, w2_words, w2_scales, offs, out):
+    nc = tc.nc
+    with ExitStack() as ctx:
+        keep = ctx.enter_context(tc.tile_pool(name="keep", bufs=1))
+        ring = ctx.enter_context(tc.tile_pool(name="ring", bufs=4))
+        psum = ctx.enter_context(tc.psum_pool(name="psum", bufs=4))
+
+        lst = keep.tile([P, S // 16], U16, name="lst")
+        nc.sync.dma_start(lst[:], offs)
+
+        table = [keep.tile([P, T], I32, name="table%d" % a, align_bytes=64) for a in range(PASSES)]
+        raw = [keep.tile([P, 4, H], F32, name="raw%d" % a, align_bytes=64) for a in range(PASSES)]
+        planes = keep.tile([P, T], U8, name="planes", align_bytes=64)
+        w2c = keep.tile([P, 2 * M], U8, name="w2c", align_bytes=64)
+        w2s = keep.tile([P, M], U8, name="w2s", align_bytes=64)
+
+        nc.vector.memset(planes[:].bitcast(I32), 0)
+        nc.gpsimd.memset(w2s[:].bitcast(I32), 0)
+
+        def load_table(a):
+            nc.sync.dma_start(table[a][:], tab[a, 0 : 512 * T].rearrange("(p w) -> p w", p=P).bitcast(I32))
+
+        def load_w1(a, h):
+            c = slice(256 * h, 256 * h + 256)
+            nc.sync.dma_start(raw[a][:, :, c], w1[512 * a : 512 * a + 512, c].rearrange("(p j) c -> p j c", j=4))
+
+        def load_scales(queue, q):
+            queue.dma_start(
+                planes[32 * q : 32 * q + 4 * PASSES, :].bitcast(I32),
+                tab[:, 512 * T + 4 * T * q : 512 * T + 4 * T * (q + 1)].rearrange("a (r t) -> a r t", r=4).bitcast(I32),
+            )
+
+        load_scales(nc.scalar, 0)
+        load_scales(nc.scalar, 1)
+        load_w1(0, 0)
+        load_w1(0, 1)
+        load_scales(nc.sync, 2)
+        load_scales(nc.sync, 3)
+        load_table(0)
+        load_table(1)
+        load_w1(1, 0)
+        load_w1(1, 1)
+        for q in range(4):
+            nc.sync.dma_start(w2s[32 * q : 32 * q + 4, :].bitcast(I32), w2_scales[0, 4 * q : 4 * q + 4, :].bitcast(I32))
+        load_table(2)
+        load_w1(2, 0)
+        load_w1(2, 1)
+        nc.sync.dma_start(w2c[:].bitcast(I32), w2_words[0].bitcast(I32))
+
+        gsc = keep.tile([P, S], U8, name="gsc", align_bytes=64)
+        words = {}
+        grouped = [keep.tile([P, 4 * H], BF16, name="grouped%d" % a, align_bytes=64) for a in range(PASSES)]
+        w1c = [keep.tile([P, H], U32, name="w1c%d" % a, align_bytes=64) for a in range(PASSES)]
+        w1s = [keep.tile([P, H], U8, name="w1s%d" % a, align_bytes=64) for a in range(PASSES)]
+        hc = keep.tile([P, S], U32, name="hc", align_bytes=64)
+        hs = keep.tile([P, S], U8, name="hs", align_bytes=64)
+
+        def gather_scales(s):
+            nc.vector.tensor_copy(gsc[:, SL * s : SL * s + SL], planes[:].indirect(lst[:, SL // 16 * s : SL // 16 * (s + 1)]))
+
+        def gather_words(a, s, tag=None):
+            words[a, s] = keep.tile([P, SL], U32, name=tag or "words%d%d" % (a, s), align_bytes=64)
+            nc.vector.tensor_copy(
+                words[a, s][:], table[a][:].bitcast(U32).indirect(lst[:, SL // 16 * s : SL // 16 * (s + 1)])
+            )
+
+        def group_w1(a, h, copy):
+            copy(
+                out=grouped[a][:].rearrange("p (t m j) -> p m t j", t=4, j=4)[:, 64 * h : 64 * h + 64],
+                in_=raw[a][:].rearrange("p j (m t) -> p m t j", t=4)[:, 64 * h : 64 * h + 64],
+            )
+
+        def quantize_w1(a):
+            nc.vector.quantize_mx(out=w1c[a][:].bitcast(E4M3), scales=w1s[a][:], in_=grouped[a][:])
+
+        def product1(bank, a, t, s, j0, n):
+            nc.tensor.matmul_mx(
+                out=bank,
+                lhsT=w1c[a][:, 128 * t : 128 * t + 128].bitcast(E4M3),
+                lhsT_scale=w1s[a][:, 128 * t : 128 * t + 128],
+                rhs=words[a, s][:, j0 : j0 + n].bitcast(E4M3),
+                rhs_scale=gsc[4 * a : P, SL * s + j0 : SL * s + j0 + n],
+                start=(a == 0),
+                stop=(a == PASSES - 1),
+            )
+
+        def quantize_h(hg, i):
+            nc.vector.quantize_mx(
+                out=hc[:, JT * i : JT * i + JT].bitcast(E4M3), scales=hs[:, JT * i : JT * i + JT], in_=hg[:]
+            )
+
+        def early_h(i):
+            s, c = divmod(i, 4)
+            hg = ring.tile([P, 4 * JT], BF16, name="hg", align_bytes=64)
+            nc.vector.tensor_copy(
+                hg[:].rearrange("p (j t) -> p j t", t=4), hrs[s][:, :, JT * c : JT * c + JT].rearrange("p t j -> p j t")
+            )
+            quantize_h(hg, i)
+
+        def late_h(i):
+            acc = psum.tile([P, 4, JT], F32, name="acc")
+            s, c = divmod(i, 4)
+            for t in range(4):
+                for a in range(PASSES):
+                    product1(acc[:, t, :], a, t, s, JT * c, JT)
+            hg = ring.tile([P, 4 * JT], BF16, name="hg", align_bytes=64)
+            nc.scalar.activation(
+                hg[:].rearrange("p (j t) -> p j t", t=4), acc[:].rearrange("p t j -> p j t"), RELU
+            )
+            quantize_h(hg, i)
+
+        def product2(i):
+            ot = ring.tile([P, M], F32, name="ot", align_bytes=64, bufs=8)
+            for n in range(2):
+                res = psum.tile([P, 512], F32, name="res")
+                nc.tensor.matmul_mx(
+                    out=res[:],
+                    lhsT=hc[:, JT * i : JT * i + JT].bitcast(E4M3),
+                    lhsT_scale=hs[:, JT * i : JT * i + JT],
+                    rhs=w2c[:, 1024 * n : 1024 * n + 1024].bitcast(E2M1),
+                    rhs_scale=w2s[:, 512 * n : 512 * n + 512],
+                    start=True,
+                    stop=True,
+                )
+                if n == 0:
+                    nc.scalar.copy(out=ot[:, 0:512], in_=res[:])
+                else:
+                    nc.vector.tensor_copy(ot[:, 512:1024], res[:])
+            nc.sync.dma_start(out[JT * i : JT * i + JT, :], ot[:])
+
+        banks = []
+        for s in range(2):
+            for t in range(4):
+                b = psum.tile([P, SL], F32, name="acc" if s == 0 else "res")
+                banks.append(b)
+        for s in range(4):
+            gather_scales(s)
+        for a in range(2):
+            group_w1(a, 0, nc.scalar.copy)
+            group_w1(a, 1, nc.scalar.copy)
+            quantize_w1(a)
+            for s in range(4):
+                gather_words(a, s)
+            for i in range(8):
+                product1(banks[i][:], a, i % 4, i // 4, 0, SL)
+        group_w1(2, 0, nc.scalar.copy)
+        group_w1(2, 1, nc.scalar.copy)
+        quantize_w1(2)
+        gather_words(2, 0)
+        gather_words(2, 1)
+        hrs = []
+        for s in range(2):
+            hr = ring.tile([P, 4, SL], BF16, name="hr", align_bytes=64)
+            hrs.append(hr)
+            for t in range(4):
+                product1(banks[4 * s + t][:], 2, t, s, 0, SL)
+                if t % 2 == 0 or s == 1:
+                    nc.scalar.activation(hr[:, t, :], banks[4 * s + t][:], RELU)
+                else:
+                    nc.vector.tensor_scalar_max(hr[:, t, :], banks[4 * s + t][:], 0.0)
+        gather_words(2, 2)
+        for i in range(4):
+            early_h(i)
+        gather_words(2, 3, tag="words20")
+        late_h(8)
+        for i in range(8):
+            if i < 4:
+                early_h(4 + i)
+            if i < 7:
+                late_h(9 + i)
+            product2(2 * i)
+            product2(2 * i + 1)

@@ -43,9 +43,10 @@ def tile_list_tabmlp_tm_none_kernel(tc, tab, w1, w2_words, w2_scales, offs, out)
         def load_table(a):
             nc.sync.dma_start(table[a][:], tab[a, 0 : 512 * T].rearrange("(p w) -> p w", p=P).bitcast(I32))
 
-        def load_w1(a, h):
-            c = slice(256 * h, 256 * h + 256)
-            nc.sync.dma_start(raw[a][:, :, c], w1[512 * a : 512 * a + 512, c].rearrange("(p j) c -> p j c", j=4))
+        def load_w1(a, c0, c1):
+            nc.sync.dma_start(
+                raw[a][:, :, c0:c1], w1[512 * a : 512 * a + 512, c0:c1].rearrange("(p j) c -> p j c", j=4)
+            )
 
         def load_scales(queue, q):
             queue.dma_start(
@@ -55,19 +56,16 @@ def tile_list_tabmlp_tm_none_kernel(tc, tab, w1, w2_words, w2_scales, offs, out)
 
         load_scales(nc.scalar, 0)
         load_scales(nc.scalar, 1)
-        load_w1(0, 0)
-        load_w1(0, 1)
+        load_table(0)
         load_scales(nc.sync, 2)
         load_scales(nc.sync, 3)
-        load_table(0)
+        load_w1(0, 0, H)
         load_table(1)
-        load_w1(1, 0)
-        load_w1(1, 1)
+        load_w1(1, 0, H)
         for q in range(4):
             nc.sync.dma_start(w2s[32 * q : 32 * q + 4, :].bitcast(I32), w2_scales[0, 4 * q : 4 * q + 4, :].bitcast(I32))
+        load_w1(2, 0, H)
         load_table(2)
-        load_w1(2, 0)
-        load_w1(2, 1)
         nc.sync.dma_start(w2c[:].bitcast(I32), w2_words[0].bitcast(I32))
 
         gsc = keep.tile([P, S], U8, name="gsc", align_bytes=64)
@@ -87,55 +85,63 @@ def tile_list_tabmlp_tm_none_kernel(tc, tab, w1, w2_words, w2_scales, offs, out)
                 words[a, s][:], table[a][:].bitcast(U32).indirect(lst[:, SL // 16 * s : SL // 16 * (s + 1)])
             )
 
-        def group_w1(a, h, copy):
+        def group_w1(a, m0, m1, copy):
             copy(
-                out=grouped[a][:].rearrange("p (t m j) -> p m t j", t=4, j=4)[:, 64 * h : 64 * h + 64],
-                in_=raw[a][:].rearrange("p j (m t) -> p m t j", t=4)[:, 64 * h : 64 * h + 64],
+                out=grouped[a][:].rearrange("p (t m j) -> p m t j", t=4, j=4)[:, m0:m1],
+                in_=raw[a][:].rearrange("p j (m t) -> p m t j", t=4)[:, m0:m1],
             )
 
-        def quantize_w1(a):
-            nc.vector.quantize_mx(out=w1c[a][:].bitcast(E4M3), scales=w1s[a][:], in_=grouped[a][:])
+        def quantize_w1(a, c0, c1):
+            nc.vector.quantize_mx(
+                out=w1c[a][:, c0:c1].bitcast(E4M3), scales=w1s[a][:, c0:c1], in_=grouped[a][:, 4 * c0 : 4 * c1]
+            )
 
-        def product1(bank, a, t, s, j0, n):
+        def relu(engine, out, in_):
+            if engine == "S":
+                nc.scalar.activation(out, in_, RELU)
+            else:
+                nc.vector.tensor_scalar_max(out, in_, 0.0)
+
+        def product1(bank, a, t, s, j0, n, first=None, last=None):
             nc.tensor.matmul_mx(
                 out=bank,
                 lhsT=w1c[a][:, 128 * t : 128 * t + 128].bitcast(E4M3),
                 lhsT_scale=w1s[a][:, 128 * t : 128 * t + 128],
                 rhs=words[a, s][:, j0 : j0 + n].bitcast(E4M3),
                 rhs_scale=gsc[4 * a : P, SL * s + j0 : SL * s + j0 + n],
-                start=(a == 0),
-                stop=(a == PASSES - 1),
+                start=(a == 0) if first is None else first,
+                stop=(a == PASSES - 1) if last is None else last,
             )
 
-        def quantize_h(hg, i):
+        def quantize_h(i):
             nc.vector.quantize_mx(
-                out=hc[:, JT * i : JT * i + JT].bitcast(E4M3), scales=hs[:, JT * i : JT * i + JT], in_=hg[:]
+                out=hc[:, JT * i : JT * i + JT].bitcast(E4M3), scales=hs[:, JT * i : JT * i + JT], in_=hgs[i][:]
             )
+
+        hgs = {}
 
         def early_h(i):
             s, c = divmod(i, 4)
-            hg = ring.tile([P, 4 * JT], BF16, name="hg", align_bytes=64)
+            hg = ring.tile([P, 4 * JT], BF16, name="hg", align_bytes=64, bufs=6)
             nc.vector.tensor_copy(
                 hg[:].rearrange("p (j t) -> p j t", t=4), hrs[s][:, :, JT * c : JT * c + JT].rearrange("p t j -> p j t")
             )
-            quantize_h(hg, i)
+            hgs[i] = hg
 
-        def late_h(i):
-            acc = psum.tile([P, 4, JT], F32, name="acc")
+        def late_h(i, engine="S"):
+            acc = psum.tile([P, 4, JT], F32, name="late")
             s, c = divmod(i, 4)
             for t in range(4):
-                for a in range(PASSES):
-                    product1(acc[:, t, :], a, t, s, JT * c, JT)
-            hg = ring.tile([P, 4 * JT], BF16, name="hg", align_bytes=64)
-            nc.scalar.activation(
-                hg[:].rearrange("p (j t) -> p j t", t=4), acc[:].rearrange("p t j -> p j t"), RELU
-            )
-            quantize_h(hg, i)
+                for a in (2, 0, 1):
+                    product1(acc[:, t, :], a, t, s, JT * c, JT, a == 2, a == 1)
+            hg = ring.tile([P, 4 * JT], BF16, name="hg", align_bytes=64, bufs=6)
+            relu(engine, hg[:].rearrange("p (j t) -> p j t", t=4), acc[:].rearrange("p t j -> p j t"))
+            hgs[i] = hg
 
-        def product2(i):
+        def product2(i, engines="SV"):
             ot = ring.tile([P, M], F32, name="ot", align_bytes=64, bufs=8)
             for n in range(2):
-                res = psum.tile([P, 512], F32, name="res")
+                res = psum.tile([P, 512], F32, name="acc")
                 nc.tensor.matmul_mx(
                     out=res[:],
                     lhsT=hc[:, JT * i : JT * i + JT].bitcast(E4M3),
@@ -145,51 +151,122 @@ def tile_list_tabmlp_tm_none_kernel(tc, tab, w1, w2_words, w2_scales, offs, out)
                     start=True,
                     stop=True,
                 )
-                if n == 0:
-                    nc.scalar.copy(out=ot[:, 0:512], in_=res[:])
+                if engines[n] == "S":
+                    nc.scalar.copy(out=ot[:, 512 * n : 512 * n + 512], in_=res[:])
                 else:
-                    nc.vector.tensor_copy(ot[:, 512:1024], res[:])
+                    nc.vector.tensor_copy(ot[:, 512 * n : 512 * n + 512], res[:])
             nc.sync.dma_start(out[JT * i : JT * i + JT, :], ot[:])
 
         banks = []
         for s in range(2):
             for t in range(4):
-                b = psum.tile([P, SL], F32, name="acc" if s == 0 else "res")
+                b = psum.tile([P, SL], F32, name="acc" if s == 0 else "late")
                 banks.append(b)
-        for s in range(4):
-            gather_scales(s)
-        for a in range(2):
-            group_w1(a, 0, nc.scalar.copy)
-            group_w1(a, 1, nc.scalar.copy)
-            quantize_w1(a)
-            for s in range(4):
-                gather_words(a, s)
-            for i in range(8):
-                product1(banks[i][:], a, i % 4, i // 4, 0, SL)
-        group_w1(2, 0, nc.scalar.copy)
-        group_w1(2, 1, nc.scalar.copy)
-        quantize_w1(2)
+        gather_scales(0)
+        gather_scales(1)
+        gather_scales(2)
+        gather_scales(3)
+        group_w1(0, 0, 128, nc.scalar.copy)
+        quantize_w1(0, 0, H)
+        gather_words(0, 0)
+        gather_words(0, 1)
+        gather_words(0, 2)
+        gather_words(0, 3)
+        product1(banks[0][:], 0, 0, 0, 0, SL)
+        product1(banks[1][:], 0, 1, 0, 0, SL)
+        product1(banks[2][:], 0, 2, 0, 0, SL)
+        product1(banks[3][:], 0, 3, 0, 0, SL)
+        product1(banks[4][:], 0, 0, 1, 0, SL)
+        product1(banks[5][:], 0, 1, 1, 0, SL)
+        product1(banks[6][:], 0, 2, 1, 0, SL)
+        product1(banks[7][:], 0, 3, 1, 0, SL)
+        gather_words(1, 0)
+        gather_words(1, 1)
+        gather_words(1, 2)
+        gather_words(1, 3)
+        group_w1(1, 0, 128, nc.scalar.copy)
+        quantize_w1(1, 0, H)
+        product1(banks[0][:], 1, 0, 0, 0, SL)
+        product1(banks[1][:], 1, 1, 0, 0, SL)
+        product1(banks[2][:], 1, 2, 0, 0, SL)
+        product1(banks[3][:], 1, 3, 0, 0, SL)
+        product1(banks[4][:], 1, 0, 1, 0, SL)
+        product1(banks[5][:], 1, 1, 1, 0, SL)
+        product1(banks[6][:], 1, 2, 1, 0, SL)
+        product1(banks[7][:], 1, 3, 1, 0, SL)
+        group_w1(2, 0, 64, nc.scalar.copy)
+        group_w1(2, 64, 128, nc.scalar.copy)
+        quantize_w1(2, 0, H)
+        hrs = [ring.tile([P, 4, SL], BF16, name="hr", align_bytes=64) for s in range(2)]
         gather_words(2, 0)
+        product1(banks[0][:], 2, 0, 0, 0, SL)
+        product1(banks[1][:], 2, 1, 0, 0, SL)
+        product1(banks[2][:], 2, 2, 0, 0, SL)
+        product1(banks[3][:], 2, 3, 0, 0, SL)
+        relu("S", hrs[0][:, 0, 0:128], banks[0][:, 0:128])
+        relu("S", hrs[0][:, 1, 0:128], banks[1][:, 0:128])
+        relu("S", hrs[0][:, 2, 0:128], banks[2][:, 0:128])
+        relu("S", hrs[0][:, 3, 0:128], banks[3][:, 0:128])
+        early_h(0)
+        quantize_h(0)
+        product2(0)
         gather_words(2, 1)
-        hrs = []
-        for s in range(2):
-            hr = ring.tile([P, 4, SL], BF16, name="hr", align_bytes=64)
-            hrs.append(hr)
-            for t in range(4):
-                product1(banks[4 * s + t][:], 2, t, s, 0, SL)
-                if t % 2 == 0 or s == 1:
-                    nc.scalar.activation(hr[:, t, :], banks[4 * s + t][:], RELU)
-                else:
-                    nc.vector.tensor_scalar_max(hr[:, t, :], banks[4 * s + t][:], 0.0)
-        gather_words(2, 2)
-        for i in range(4):
-            early_h(i)
-        gather_words(2, 3, tag="words20")
+        product1(banks[4][:], 2, 0, 1, 0, SL)
+        product1(banks[5][:], 2, 1, 1, 0, SL)
+        product1(banks[6][:], 2, 2, 1, 0, SL)
+        product1(banks[7][:], 2, 3, 1, 0, SL)
+        relu("S", hrs[0][:, 0, 128:512], banks[0][:, 128:512])
+        relu("V", hrs[0][:, 1, 128:512], banks[1][:, 128:512])
+        relu("S", hrs[0][:, 2, 128:512], banks[2][:, 128:512])
+        relu("V", hrs[0][:, 3, 128:512], banks[3][:, 128:512])
+        early_h(1)
+        early_h(2)
+        quantize_h(1)
+        product2(1)
+        early_h(3)
+        quantize_h(2)
+        product2(2)
+        quantize_h(3)
+        relu("S", hrs[1][:, 0, 0:SL], banks[4][:, 0:SL])
+        relu("S", hrs[1][:, 1, 0:SL], banks[5][:, 0:SL])
+        product2(3)
+        gather_words(2, 2, tag="words20")
+        relu("S", hrs[1][:, 2, 0:SL], banks[6][:, 0:SL])
+        relu("S", hrs[1][:, 3, 0:SL], banks[7][:, 0:SL])
+        early_h(4)
+        early_h(5)
+        quantize_h(4)
         late_h(8)
-        for i in range(8):
-            if i < 4:
-                early_h(4 + i)
-            if i < 7:
-                late_h(9 + i)
-            product2(2 * i)
-            product2(2 * i + 1)
+        product2(4)
+        early_h(6)
+        quantize_h(5)
+        product2(5)
+        early_h(7)
+        quantize_h(6)
+        gather_words(2, 3, tag="words21")
+        quantize_h(8)
+        quantize_h(7)
+        late_h(9)
+        product2(6)
+        late_h(10)
+        product2(7)
+        quantize_h(9)
+        product2(8)
+        late_h(11)
+        quantize_h(10)
+        product2(9)
+        late_h(12)
+        quantize_h(11)
+        product2(10)
+        late_h(13)
+        quantize_h(12)
+        product2(11)
+        late_h(14)
+        quantize_h(13)
+        product2(12)
+        late_h(15)
+        quantize_h(14)
+        product2(13)
+        quantize_h(15)
+        product2(14)
+        product2(15)

from contextlib import ExitStack

import concourse.mybir as mybir

K, H, M, T, S = 1536, 512, 1024, 4096, 2048
FLOPS = 2 * S * (K * H + H * M)

F32 = mybir.dt.float32
BF16 = mybir.dt.bfloat16
I32 = mybir.dt.int32
U32 = mybir.dt.uint32
U16 = mybir.dt.uint16
U8 = mybir.dt.uint8
E4M3 = mybir.dt.float8_e4m3fn_x4
E2M1 = mybir.dt.float4_e2m1fn_x4
RELU = mybir.ActivationFunctionType.Relu

P = 128
PASSES = K // 512
SL = 512
JT = 128


def tile_list_tabmlp_tm_none_kernel(tc, tab, w1, w2_words, w2_scales, offs, out):
    nc = tc.nc
    with ExitStack() as ctx:
        keep = ctx.enter_context(tc.tile_pool(name="keep", bufs=1))
        ring = ctx.enter_context(tc.tile_pool(name="ring", bufs=4))
        psum = ctx.enter_context(tc.psum_pool(name="psum", bufs=4))

        lst = keep.tile([P, S // 16], U16, name="lst")
        nc.sync.dma_start(lst[:], offs)

        table = [keep.tile([P, T], I32, name="table%d" % a, align_bytes=64) for a in range(PASSES)]
        raw = [keep.tile([P, 4, H], F32, name="raw%d" % a, align_bytes=64) for a in range(PASSES)]
        planes = keep.tile([P, T], U8, name="planes", align_bytes=64)
        w2c = keep.tile([P, 2 * M], U8, name="w2c", align_bytes=64)
        w2s = keep.tile([P, M], U8, name="w2s", align_bytes=64)

        nc.vector.memset(planes[:].bitcast(I32), 0)
        nc.gpsimd.memset(w2s[:].bitcast(I32), 0)

        def load_table(a):
            nc.sync.dma_start(table[a][:], tab[a, 0 : 512 * T].rearrange("(p w) -> p w", p=P).bitcast(I32))

        def load_w1(a, c0, c1):
            nc.sync.dma_start(
                raw[a][:, :, c0:c1], w1[512 * a : 512 * a + 512, c0:c1].rearrange("(p j) c -> p j c", j=4)
            )

        def load_scales(queue, q):
            queue.dma_start(
                planes[32 * q : 32 * q + 4 * PASSES, :].bitcast(I32),
                tab[:, 512 * T + 4 * T * q : 512 * T + 4 * T * (q + 1)].rearrange("a (r t) -> a r t", r=4).bitcast(I32),
            )

        load_scales(nc.scalar, 0)
        load_scales(nc.scalar, 1)
        load_table(0)
        load_scales(nc.sync, 2)
        load_scales(nc.sync, 3)
        load_w1(0, 0, H)
        load_table(1)
        load_w1(1, 0, H)
        for q in range(4):
            nc.sync.dma_start(w2s[32 * q : 32 * q + 4, :].bitcast(I32), w2_scales[0, 4 * q : 4 * q + 4, :].bitcast(I32))
        load_w1(2, 0, H)
        load_table(2)
        nc.sync.dma_start(w2c[:].bitcast(I32), w2_words[0].bitcast(I32))

        gsc = keep.tile([P, S], U8, name="gsc", align_bytes=64)
        words = {}
        grouped = [keep.tile([P, 4 * H], BF16, name="grouped%d" % a, align_bytes=64) for a in range(PASSES)]
        w1c = [keep.tile([P, H], U32, name="w1c%d" % a, align_bytes=64) for a in range(PASSES)]
        w1s = [keep.tile([P, H], U8, name="w1s%d" % a, align_bytes=64) for a in range(PASSES)]
        hc = keep.tile([P, S], U32, name="hc", align_bytes=64)
        hs = keep.tile([P, S], U8, name="hs", align_bytes=64)

        def gather_scales(s):
            nc.vector.tensor_copy(gsc[:, SL * s : SL * s + SL], planes[:].indirect(lst[:, SL // 16 * s : SL // 16 * (s + 1)]))

        def gather_words(a, s, tag=None):
            words[a, s] = keep.tile([P, SL], U32, name=tag or "words%d%d" % (a, s), align_bytes=64)
            nc.vector.tensor_copy(
                words[a, s][:], table[a][:].bitcast(U32).indirect(lst[:, SL // 16 * s : SL // 16 * (s + 1)])
            )

        def group_w1(a, m0, m1, copy):
            copy(
                out=grouped[a][:].rearrange("p (t m j) -> p m t j", t=4, j=4)[:, m0:m1],
                in_=raw[a][:].rearrange("p j (m t) -> p m t j", t=4)[:, m0:m1],
            )

        def quantize_w1(a, c0, c1):
            nc.vector.quantize_mx(
                out=w1c[a][:, c0:c1].bitcast(E4M3), scales=w1s[a][:, c0:c1], in_=grouped[a][:, 4 * c0 : 4 * c1]
            )

        def relu(engine, out, in_):
            if engine == "S":
                nc.scalar.activation(out, in_, RELU)
            else:
                nc.vector.tensor_scalar_max(out, in_, 0.0)

        def product1(bank, a, t, s, j0, n, first=None, last=None):
            nc.tensor.matmul_mx(
                out=bank,
                lhsT=w1c[a][:, 128 * t : 128 * t + 128].bitcast(E4M3),
                lhsT_scale=w1s[a][:, 128 * t : 128 * t + 128],
                rhs=words[a, s][:, j0 : j0 + n].bitcast(E4M3),
                rhs_scale=gsc[4 * a : P, SL * s + j0 : SL * s + j0 + n],
                start=(a == 0) if first is None else first,
                stop=(a == PASSES - 1) if last is None else last,
            )

        def quantize_h(i):
            nc.vector.quantize_mx(
                out=hc[:, JT * i : JT * i + JT].bitcast(E4M3), scales=hs[:, JT * i : JT * i + JT], in_=hgs[i][:]
            )

        hgs = {}

        def early_h(i):
            s, c = divmod(i, 4)
            hg = ring.tile([P, 4 * JT], BF16, name="hg", align_bytes=64, bufs=6)
            nc.vector.tensor_copy(
                hg[:].rearrange("p (j t) -> p j t", t=4), hrs[s][:, :, JT * c : JT * c + JT].rearrange("p t j -> p j t")
            )
            hgs[i] = hg

        def late_h(i, engine="S"):
            acc = psum.tile([P, 4, JT], F32, name="late")
            s, c = divmod(i, 4)
            for t in range(4):
                for a in (2, 0, 1):
                    product1(acc[:, t, :], a, t, s, JT * c, JT, a == 2, a == 1)
            hg = ring.tile([P, 4 * JT], BF16, name="hg", align_bytes=64, bufs=6)
            relu(engine, hg[:].rearrange("p (j t) -> p j t", t=4), acc[:].rearrange("p t j -> p j t"))
            hgs[i] = hg

        def product2(i, engines="SV"):
            ot = ring.tile([P, M], F32, name="ot", align_bytes=64, bufs=8)
            for n in range(2):
                res = psum.tile([P, 512], F32, name="acc")
                nc.tensor.matmul_mx(
                    out=res[:],
                    lhsT=hc[:, JT * i : JT * i + JT].bitcast(E4M3),
                    lhsT_scale=hs[:, JT * i : JT * i + JT],
                    rhs=w2c[:, 1024 * n : 1024 * n + 1024].bitcast(E2M1),
                    rhs_scale=w2s[:, 512 * n : 512 * n + 512],
                    start=True,
                    stop=True,
                )
                if engines[n] == "S":
                    nc.scalar.copy(out=ot[:, 512 * n : 512 * n + 512], in_=res[:])
                else:
                    nc.vector.tensor_copy(ot[:, 512 * n : 512 * n + 512], res[:])
            nc.sync.dma_start(out[JT * i : JT * i + JT, :], ot[:])

        banks = []
        for s in range(2):
            for t in range(4):
                b = psum.tile([P, SL], F32, name="acc" if s == 0 else "late")
                banks.append(b)
        gather_scales(0)
        gather_scales(1)
        gather_scales(2)
        gather_scales(3)
        group_w1(0, 0, 128, nc.scalar.copy)
        quantize_w1(0, 0, H)
        gather_words(0, 0)
        gather_words(0, 1)
        gather_words(0, 2)
        gather_words(0, 3)
        product1(banks[0][:], 0, 0, 0, 0, SL)
        product1(banks[1][:], 0, 1, 0, 0, SL)
        product1(banks[2][:], 0, 2, 0, 0, SL)
        product1(banks[3][:], 0, 3, 0, 0, SL)
        product1(banks[4][:], 0, 0, 1, 0, SL)
        product1(banks[5][:], 0, 1, 1, 0, SL)
        product1(banks[6][:], 0, 2, 1, 0, SL)
        product1(banks[7][:], 0, 3, 1, 0, SL)
        gather_words(1, 0)
        gather_words(1, 1)
        gather_words(1, 2)
        gather_words(1, 3)
        group_w1(1, 0, 128, nc.scalar.copy)
        quantize_w1(1, 0, H)
        product1(banks[0][:], 1, 0, 0, 0, SL)
        product1(banks[1][:], 1, 1, 0, 0, SL)
        product1(banks[2][:], 1, 2, 0, 0, SL)
        product1(banks[3][:], 1, 3, 0, 0, SL)
        product1(banks[4][:], 1, 0, 1, 0, SL)
        product1(banks[5][:], 1, 1, 1, 0, SL)
        product1(banks[6][:], 1, 2, 1, 0, SL)
        product1(banks[7][:], 1, 3, 1, 0, SL)
        group_w1(2, 0, 64, nc.scalar.copy)
        group_w1(2, 64, 128, nc.scalar.copy)
        quantize_w1(2, 0, H)
        hrs = [ring.tile([P, 4, SL], BF16, name="hr", align_bytes=64) for s in range(2)]
        gather_words(2, 0)
        product1(banks[0][:], 2, 0, 0, 0, SL)
        product1(banks[1][:], 2, 1, 0, 0, SL)
        product1(banks[2][:], 2, 2, 0, 0, SL)
        product1(banks[3][:], 2, 3, 0, 0, SL)
        relu("S", hrs[0][:, 0, 0:128], banks[0][:, 0:128])
        relu("S", hrs[0][:, 1, 0:128], banks[1][:, 0:128])
        relu("S", hrs[0][:, 2, 0:128], banks[2][:, 0:128])
        relu("S", hrs[0][:, 3, 0:128], banks[3][:, 0:128])
        early_h(0)
        quantize_h(0)
        product2(0)
        gather_words(2, 1)
        product1(banks[4][:], 2, 0, 1, 0, SL)
        product1(banks[5][:], 2, 1, 1, 0, SL)
        product1(banks[6][:], 2, 2, 1, 0, SL)
        product1(banks[7][:], 2, 3, 1, 0, SL)
        relu("S", hrs[0][:, 0, 128:512], banks[0][:, 128:512])
        relu("V", hrs[0][:, 1, 128:512], banks[1][:, 128:512])
        relu("S", hrs[0][:, 2, 128:512], banks[2][:, 128:512])
        relu("V", hrs[0][:, 3, 128:512], banks[3][:, 128:512])
        early_h(1)
        early_h(2)
        quantize_h(1)
        product2(1)
        early_h(3)
        quantize_h(2)
        product2(2)
        quantize_h(3)
        relu("S", hrs[1][:, 0, 0:SL], banks[4][:, 0:SL])
        relu("S", hrs[1][:, 1, 0:SL], banks[5][:, 0:SL])
        product2(3)
        gather_words(2, 2, tag="words20")
        relu("S", hrs[1][:, 2, 0:SL], banks[6][:, 0:SL])
        relu("S", hrs[1][:, 3, 0:SL], banks[7][:, 0:SL])
        early_h(4)
        early_h(5)
        quantize_h(4)
        late_h(8)
        product2(4)
        early_h(6)
        quantize_h(5)
        product2(5)
        early_h(7)
        quantize_h(6)
        gather_words(2, 3, tag="words21")
        quantize_h(8)
        quantize_h(7)
        late_h(9)
        product2(6)
        late_h(10)
        product2(7)
        quantize_h(9)
        product2(8)
        late_h(11)
        quantize_h(10)
        product2(9)
        late_h(12)
        quantize_h(11)
        product2(10)
        late_h(13)
        quantize_h(12)
        product2(11)
        late_h(14)
        quantize_h(13)
        product2(12)
        late_h(15)
        quantize_h(14)
        product2(13)
        quantize_h(15)
        product2(14)
        product2(15)
